import numpy as np
import ml_dtypes


def mxq(x, axis, fmt="e4m3"):
    dtype, down = {"e4m3": (ml_dtypes.float8_e4m3fn, 7), "e5m2": (ml_dtypes.float8_e5m2, 14)}[fmt]
    v = np.moveaxis(np.asarray(x, np.float32).astype(ml_dtypes.bfloat16).astype(np.float64), axis, -1)
    blocks = v.reshape(v.shape[:-1] + (-1, 32))
    amax = np.abs(blocks).max(-1, keepdims=True)
    byte = np.maximum(np.where(amax > 0, np.frexp(amax)[1] - 1 + 127, 0) - down, 1)
    scale = np.exp2(byte - 127.0)
    codes = (blocks / scale).astype(np.float32).astype(dtype).astype(np.float64)
    return np.moveaxis((codes * scale).reshape(v.shape), -1, axis)


WIDE = False


def mx_kscale(k, group=512):
    if not WIDE:
        return np.ones(k)
    levels = np.array([10, -10, 5, -5, 0])
    if group != 512:
        return np.exp2(np.random.permutation(np.resize(levels, k // group))).repeat(group)
    if k % 512:
        return np.exp2(np.random.permutation(np.resize(levels, k // 32))).repeat(32)
    a = np.empty((k // 512, 16))
    for p in range(k // 512):
        a[p, :8] = np.random.permutation(np.resize(levels, 8))
        for g in range(8):
            far = levels[np.abs(levels - a[p, g]) >= 10]
            a[p, g + 8] = far[np.random.randint(len(far))]
    return np.exp2(a.ravel()).repeat(32)


def f64(x):
    return np.asarray(x).astype(np.float64)


E2M1 = np.array([0.0, 0.5, 1.0, 1.5, 2.0, 3.0, 4.0, 6.0, -0.0, -0.5, -1.0, -1.5, -2.0, -3.0, -4.0, -6.0])


def pack_group(w):
    k, n = w.shape
    w = f64(np.asarray(w, np.float32).astype(ml_dtypes.bfloat16)).reshape(k // 32, 32, n)
    amax = np.abs(w).max(1)
    mant, ex = np.frexp(amax / 6.0)
    byte = np.clip(np.where(amax > 0, np.where(mant > 0.5, ex, ex - 1) + 127, 1), 1, 254)
    scaled = (w * np.exp2(127.0 - byte)[:, None, :]).reshape(k, n).astype(np.float32)
    c = np.ascontiguousarray(scaled.reshape(k // 4, 4, n).transpose(0, 2, 1)).astype(ml_dtypes.float4_e2m1fn).view(np.uint8) & 0xF
    return np.ascontiguousarray((c[..., 0::2] | (c[..., 1::2] << 4)).reshape(k // 4, 2 * n)), byte.astype(np.uint8)


def unpack_group(words, scales):
    p, n = words.shape[0], scales.shape[1]
    words = np.ascontiguousarray(words).reshape(p, n, 2)
    nib = np.empty((p, n, 4), np.uint8)
    nib[..., 0::2] = words & 0xF
    nib[..., 1::2] = words >> 4
    return E2M1[nib].transpose(0, 2, 1).reshape(4 * p, n) * np.repeat(np.exp2(scales.astype(np.float64) - 127.0), 32, axis=0)


G, D, M, N = 4, 256, 256, 512


def setup_inputs():
    n = np.random.standard_normal
    s = mx_kscale(D, 0)[:, None]
    w_ = [pack_group(w) for w in n((G, D, M)) / np.sqrt(D) / s]
    return {
        "x": (n((G, D, N)) * s).astype(np.float32),
        "w_words": np.stack([w[0] for w in w_]),
        "w_scales": np.stack([w[1] for w in w_]),
        "b": (0.5 * n((G, M, 1))).astype(np.float32),
        "r": n((G, M, N)).astype(np.float32),
    }


def reference(x, w_words, w_scales, b, r):
    xq = mxq(f64(x), 1, "e4m3")
    y = np.stack([unpack_group(w_words[g], w_scales[g]) for g in range(G)]).transpose(0, 2, 1) @ xq
    y = y + f64(b)
    y = y + f64(r)
    return y

@@ -1,0 +1,132 @@
+from contextlib import ExitStack
+
+import concourse.mybir as mybir
+
+G, D, M, N = 4, 256, 256, 512
+FLOPS = 2 * G * D * M * N
+
+F32 = mybir.dt.float32
+BF16 = mybir.dt.bfloat16
+I32 = mybir.dt.int32
+U32 = mybir.dt.uint32
+U8 = mybir.dt.uint8
+FP8X4 = mybir.dt.float8_e4m3fn_x4
+FP4X4 = mybir.dt.float4_e2m1fn_x4
+ADD = mybir.AluOpType.add
+
+P = 128
+PACK = 4
+ROWS = D // PACK
+SIDE = P // ROWS
+PAIRS = G // SIDE
+HALVES = M // P
+QUAD = 32
+SCALE_ROWS = 4
+VECTOR_COLUMNS = 344
+RUN = 4
+
+
+def tile_rows_glin_bias_res_kernel(tc, x, w_words, w_scales, b, r, out):
+    nc = tc.nc
+    with ExitStack() as ctx:
+        sb = ctx.enter_context(tc.tile_pool(name="sb", bufs=1))
+        ps = ctx.enter_context(tc.psum_pool(name="ps", bufs=1))
+        ctx.enter_context(tc.manual_schedule())
+
+        w_raw = sb.tile([P, PAIRS, 2 * M], U8, name="w_raw", align_bytes=64)
+        s_raw = sb.tile([P, PAIRS, M], U8, name="s_raw", align_bytes=64)
+        w_dealt = [sb.tile([P, HALVES, 2 * P], U8, name="w_dealt%d" % h, align_bytes=64) for h in range(PAIRS)]
+        s_dealt = [sb.tile([P, HALVES, P], U8, name="s_dealt%d" % h, align_bytes=64) for h in range(PAIRS)]
+        bias = sb.tile([P, G, 8], F32, name="bias")
+        x_raw = [sb.tile([P, PACK, N], F32, name="x_raw%d" % h, align_bytes=64) for h in range(PAIRS)]
+        x_bf = [sb.tile([P, N, PACK], BF16, name="x_bf%d" % h, align_bytes=64) for h in range(PAIRS)]
+        x_codes = [sb.tile([P, N], U32, name="x_codes%d" % h, align_bytes=64) for h in range(PAIRS)]
+        x_scales = [sb.tile([P, N], U8, name="x_scales%d" % h, align_bytes=64) for h in range(PAIRS)]
+        res = [sb.tile([P, HALVES, N], F32, name="res%d" % g, align_bytes=64) for g in range(G)]
+        y = [sb.tile([P, HALVES, N], F32, name="y%d" % g, align_bytes=64) for g in range(G)]
+        acc = [[ps.tile([P, N], F32, name="acc%d_%d" % (g, t)) for t in range(HALVES)] for g in range(G)]
+
+        nc.vector.memset(s_raw[:].bitcast(I32), 0)
+
+        nc.scalar.dma_start(
+            out=w_raw[:].bitcast(I32),
+            in_=w_words.bitcast(I32).rearrange("(h c) q n -> (c q) h n", c=SIDE),
+        )
+        scale_rows = w_scales.bitcast(I32).rearrange("(h c) (u i) n -> i (c u) h n", c=SIDE, i=SCALE_ROWS)
+        for i in range(SCALE_ROWS):
+            nc.scalar.dma_start(out=s_raw[i:P:QUAD, :, :].bitcast(I32), in_=scale_rows[i])
+        nc.scalar.dma_start(out=bias[:, :, 0:HALVES], in_=b.rearrange("g (p t) o -> p g (t o)", t=HALVES))
+
+        x_pairs = x.rearrange("(h c) (q j) n -> h (c q) j n", c=SIDE, j=PACK)
+        for h in range(PAIRS):
+            nc.sync.dma_start(out=x_raw[h][:], in_=x_pairs[h])
+        for g in range(G):
+            nc.sync.dma_start(out=res[g][:], in_=r[g].rearrange("(p t) n -> p t n", t=HALVES))
+
+        def deal_words(h):
+            nc.vector.tensor_copy(
+                out=w_dealt[h][:].rearrange("p t (m e) -> p t m e", e=2),
+                in_=w_raw[:, h, :].rearrange("p (m t e) -> p t m e", t=HALVES, e=2),
+            )
+
+        def deal_scales(h):
+            nc.vector.tensor_copy(
+                out=s_dealt[h][:],
+                in_=s_raw[:, h, :].rearrange("p (m t) -> p t m", t=HALVES),
+            )
+
+        def interleave(h):
+            for copy, cols in (
+                (nc.vector.tensor_copy, slice(0, VECTOR_COLUMNS)),
+                (nc.scalar.copy, slice(VECTOR_COLUMNS, N)),
+            ):
+                copy(
+                    out=x_bf[h][:, cols, :].rearrange("p (c i) j -> p c j i", i=RUN),
+                    in_=x_raw[h][:, :, cols].rearrange("p j (c i) -> p c j i", i=RUN),
+                )
+
+        def quantize(h):
+            nc.vector.quantize_mx(
+                out=x_codes[h][:].bitcast(FP8X4),
+                scales=x_scales[h][:],
+                in_=x_bf[h][:].rearrange("p n j -> p (n j)"),
+            )
+
+        def multiply(h):
+            for t in range(HALVES):
+                for c in range(SIDE):
+                    rows = slice(ROWS * c, ROWS * (c + 1))
+                    nc.tensor.matmul_mx(
+                        out=acc[SIDE * h + c][t][:],
+                        lhsT=w_dealt[h][rows, t, :].bitcast(FP4X4),
+                        lhsT_scale=s_dealt[h][rows, t, :],
+                        rhs=x_codes[h][rows, :].bitcast(FP8X4),
+                        rhs_scale=x_scales[h][rows, :],
+                        start=True,
+                        stop=True,
+                    )
+
+        def finish(g):
+            for t in range(HALVES):
+                nc.vector.scalar_tensor_tensor(
+                    out=y[g][:, t, :],
+                    in0=acc[g][t][:],
+                    scalar=bias[:, g, t : t + 1],
+                    in1=res[g][:, t, :],
+                    op0=ADD,
+                    op1=ADD,
+                )
+            nc.sync.dma_start(out=out[g].rearrange("(p t) n -> p t n", t=HALVES), in_=y[g][:])
+
+        deal_words(0)
+        deal_scales(0)
+        interleave(0)
+        deal_words(1)
+        quantize(0)
+        multiply(0)
+        interleave(1)
+        deal_scales(1)
+        quantize(1)
+        multiply(1)
+        for g in range(G):
+            finish(g)

@@ -48,18 +48,18 @@ def tile_rows_glin_bias_res_kernel(tc, x, w_words, w_scales, b, r, out):
 
         nc.vector.memset(s_raw[:].bitcast(I32), 0)
 
-        nc.scalar.dma_start(
+        x_pairs = x.rearrange("(h c) (q j) n -> h (c q) j n", c=SIDE, j=PACK)
+        nc.sync.dma_start(out=x_raw[0][:], in_=x_pairs[0])
+        nc.sync.dma_start(
             out=w_raw[:].bitcast(I32),
             in_=w_words.bitcast(I32).rearrange("(h c) q n -> (c q) h n", c=SIDE),
         )
         scale_rows = w_scales.bitcast(I32).rearrange("(h c) (u i) n -> i (c u) h n", c=SIDE, i=SCALE_ROWS)
         for i in range(SCALE_ROWS):
-            nc.scalar.dma_start(out=s_raw[i:P:QUAD, :, :].bitcast(I32), in_=scale_rows[i])
-        nc.scalar.dma_start(out=bias[:, :, 0:HALVES], in_=b.rearrange("g (p t) o -> p g (t o)", t=HALVES))
+            nc.sync.dma_start(out=s_raw[i:P:QUAD, :, :].bitcast(I32), in_=scale_rows[i])
 
-        x_pairs = x.rearrange("(h c) (q j) n -> h (c q) j n", c=SIDE, j=PACK)
-        for h in range(PAIRS):
-            nc.sync.dma_start(out=x_raw[h][:], in_=x_pairs[h])
+        nc.sync.dma_start(out=x_raw[1][:], in_=x_pairs[1])
+        nc.sync.dma_start(out=bias[:, :, 0:HALVES], in_=b.rearrange("g (p t) o -> p g (t o)", t=HALVES))
         for g in range(G):
             nc.sync.dma_start(out=res[g][:], in_=r[g].rearrange("(p t) n -> p t n", t=HALVES))
 
@@ -118,12 +118,12 @@ def tile_rows_glin_bias_res_kernel(tc, x, w_words, w_scales, b, r, out):
                 )
             nc.sync.dma_start(out=out[g].rearrange("(p t) n -> p t n", t=HALVES), in_=y[g][:])
 
-        deal_words(0)
-        deal_scales(0)
         interleave(0)
-        deal_words(1)
+        deal_words(0)
         quantize(0)
+        deal_scales(0)
         multiply(0)
+        deal_words(1)
         interleave(1)
         deal_scales(1)
         quantize(1)

@@ -22,8 +22,9 @@ PAIRS = G // SIDE
 HALVES = M // P
 QUAD = 32
 SCALE_ROWS = 4
-VECTOR_COLUMNS = 344
+VECTOR_COLUMNS = (256, 344)
 RUN = 4
+B_STEP = QUAD // G
 
 
 def tile_rows_glin_bias_res_kernel(tc, x, w_words, w_scales, b, r, out):
@@ -37,7 +38,9 @@ def tile_rows_glin_bias_res_kernel(tc, x, w_words, w_scales, b, r, out):
         s_raw = sb.tile([P, PAIRS, M], U8, name="s_raw", align_bytes=64)
         w_dealt = [sb.tile([P, HALVES, 2 * P], U8, name="w_dealt%d" % h, align_bytes=64) for h in range(PAIRS)]
         s_dealt = [sb.tile([P, HALVES, P], U8, name="s_dealt%d" % h, align_bytes=64) for h in range(PAIRS)]
-        bias = sb.tile([P, G, 8], F32, name="bias")
+        b_raw = sb.tile([P, HALVES * QUAD], F32, name="b_raw", align_bytes=64)
+        b_split = sb.tile([P, HALVES, QUAD], F32, name="b_split", align_bytes=64)
+        bias = sb.tile([P, HALVES, QUAD], F32, name="bias", align_bytes=64)
         x_raw = [sb.tile([P, PACK, N], F32, name="x_raw%d" % h, align_bytes=64) for h in range(PAIRS)]
         x_bf = [sb.tile([P, N, PACK], BF16, name="x_bf%d" % h, align_bytes=64) for h in range(PAIRS)]
         x_codes = [sb.tile([P, N], U32, name="x_codes%d" % h, align_bytes=64) for h in range(PAIRS)]
@@ -47,6 +50,7 @@ def tile_rows_glin_bias_res_kernel(tc, x, w_words, w_scales, b, r, out):
         acc = [[ps.tile([P, N], F32, name="acc%d_%d" % (g, t)) for t in range(HALVES)] for g in range(G)]
 
         nc.vector.memset(s_raw[:].bitcast(I32), 0)
+        nc.vector.memset(b_raw[:], 0.0)
 
         x_pairs = x.rearrange("(h c) (q j) n -> h (c q) j n", c=SIDE, j=PACK)
         nc.sync.dma_start(out=x_raw[0][:], in_=x_pairs[0])
@@ -57,9 +61,10 @@ def tile_rows_glin_bias_res_kernel(tc, x, w_words, w_scales, b, r, out):
         scale_rows = w_scales.bitcast(I32).rearrange("(h c) (u i) n -> i (c u) h n", c=SIDE, i=SCALE_ROWS)
         for i in range(SCALE_ROWS):
             nc.sync.dma_start(out=s_raw[i:P:QUAD, :, :].bitcast(I32), in_=scale_rows[i])
-
+        nc.sync.dma_start(
+            out=b_raw[0:P:B_STEP, :], in_=b.rearrange("g (u c) o -> u g (c o)", u=P // QUAD)
+        )
         nc.sync.dma_start(out=x_raw[1][:], in_=x_pairs[1])
-        nc.sync.dma_start(out=bias[:, :, 0:HALVES], in_=b.rearrange("g (p t) o -> p g (t o)", t=HALVES))
         for g in range(G):
             nc.sync.dma_start(out=res[g][:], in_=r[g].rearrange("(p t) n -> p t n", t=HALVES))
 
@@ -75,10 +80,17 @@ def tile_rows_glin_bias_res_kernel(tc, x, w_words, w_scales, b, r, out):
                 in_=s_raw[:, h, :].rearrange("p (m t) -> p t m", t=HALVES),
             )
 
+        def split_bias():
+            nc.scalar.copy(out=b_split[:], in_=b_raw[:].rearrange("p (c t) -> p t c", t=HALVES))
+
+        def turn_bias():
+            for t in range(HALVES):
+                nc.vector.transpose(out=bias[:, t, :], in_=b_split[:, t, :])
+
         def interleave(h):
             for copy, cols in (
-                (nc.vector.tensor_copy, slice(0, VECTOR_COLUMNS)),
-                (nc.scalar.copy, slice(VECTOR_COLUMNS, N)),
+                (nc.vector.tensor_copy, slice(0, VECTOR_COLUMNS[h])),
+                (nc.scalar.copy, slice(VECTOR_COLUMNS[h], N)),
             ):
                 copy(
                     out=x_bf[h][:, cols, :].rearrange("p (c i) j -> p c j i", i=RUN),
@@ -111,7 +123,7 @@ def tile_rows_glin_bias_res_kernel(tc, x, w_words, w_scales, b, r, out):
                 nc.vector.scalar_tensor_tensor(
                     out=y[g][:, t, :],
                     in0=acc[g][t][:],
-                    scalar=bias[:, g, t : t + 1],
+                    scalar=bias[:, t, B_STEP * g : B_STEP * g + 1],
                     in1=res[g][:, t, :],
                     op0=ADD,
                     op1=ADD,
@@ -119,13 +131,15 @@ def tile_rows_glin_bias_res_kernel(tc, x, w_words, w_scales, b, r, out):
             nc.sync.dma_start(out=out[g].rearrange("(p t) n -> p t n", t=HALVES), in_=y[g][:])
 
         interleave(0)
+        split_bias()
         deal_words(0)
-        quantize(0)
         deal_scales(0)
+        quantize(0)
         multiply(0)
         deal_words(1)
-        interleave(1)
         deal_scales(1)
+        interleave(1)
+        turn_bias()
         quantize(1)
         multiply(1)
         for g in range(G):

from contextlib import ExitStack

import concourse.mybir as mybir

G, D, M, N = 4, 256, 256, 512
FLOPS = 2 * G * D * M * N

F32 = mybir.dt.float32
BF16 = mybir.dt.bfloat16
I32 = mybir.dt.int32
U32 = mybir.dt.uint32
U8 = mybir.dt.uint8
FP8X4 = mybir.dt.float8_e4m3fn_x4
FP4X4 = mybir.dt.float4_e2m1fn_x4
ADD = mybir.AluOpType.add

P = 128
PACK = 4
ROWS = D // PACK
SIDE = P // ROWS
PAIRS = G // SIDE
HALVES = M // P
QUAD = 32
SCALE_ROWS = 4
VECTOR_COLUMNS = (256, 344)
RUN = 4
B_STEP = QUAD // G


def tile_rows_glin_bias_res_kernel(tc, x, w_words, w_scales, b, r, out):
    nc = tc.nc
    with ExitStack() as ctx:
        sb = ctx.enter_context(tc.tile_pool(name="sb", bufs=1))
        ps = ctx.enter_context(tc.psum_pool(name="ps", bufs=1))
        ctx.enter_context(tc.manual_schedule())

        w_raw = sb.tile([P, PAIRS, 2 * M], U8, name="w_raw", align_bytes=64)
        s_raw = sb.tile([P, PAIRS, M], U8, name="s_raw", align_bytes=64)
        w_dealt = [sb.tile([P, HALVES, 2 * P], U8, name="w_dealt%d" % h, align_bytes=64) for h in range(PAIRS)]
        s_dealt = [sb.tile([P, HALVES, P], U8, name="s_dealt%d" % h, align_bytes=64) for h in range(PAIRS)]
        b_raw = sb.tile([P, HALVES * QUAD], F32, name="b_raw", align_bytes=64)
        b_split = sb.tile([P, HALVES, QUAD], F32, name="b_split", align_bytes=64)
        bias = sb.tile([P, HALVES, QUAD], F32, name="bias", align_bytes=64)
        x_raw = [sb.tile([P, PACK, N], F32, name="x_raw%d" % h, align_bytes=64) for h in range(PAIRS)]
        x_bf = [sb.tile([P, N, PACK], BF16, name="x_bf%d" % h, align_bytes=64) for h in range(PAIRS)]
        x_codes = [sb.tile([P, N], U32, name="x_codes%d" % h, align_bytes=64) for h in range(PAIRS)]
        x_scales = [sb.tile([P, N], U8, name="x_scales%d" % h, align_bytes=64) for h in range(PAIRS)]
        res = [sb.tile([P, HALVES, N], F32, name="res%d" % g, align_bytes=64) for g in range(G)]
        y = [sb.tile([P, HALVES, N], F32, name="y%d" % g, align_bytes=64) for g in range(G)]
        acc = [[ps.tile([P, N], F32, name="acc%d_%d" % (g, t)) for t in range(HALVES)] for g in range(G)]

        nc.vector.memset(s_raw[:].bitcast(I32), 0)
        nc.vector.memset(b_raw[:], 0.0)

        x_pairs = x.rearrange("(h c) (q j) n -> h (c q) j n", c=SIDE, j=PACK)
        nc.sync.dma_start(out=x_raw[0][:], in_=x_pairs[0])
        nc.sync.dma_start(
            out=w_raw[:].bitcast(I32),
            in_=w_words.bitcast(I32).rearrange("(h c) q n -> (c q) h n", c=SIDE),
        )
        scale_rows = w_scales.bitcast(I32).rearrange("(h c) (u i) n -> i (c u) h n", c=SIDE, i=SCALE_ROWS)
        for i in range(SCALE_ROWS):
            nc.sync.dma_start(out=s_raw[i:P:QUAD, :, :].bitcast(I32), in_=scale_rows[i])
        nc.sync.dma_start(
            out=b_raw[0:P:B_STEP, :], in_=b.rearrange("g (u c) o -> u g (c o)", u=P // QUAD)
        )
        nc.sync.dma_start(out=x_raw[1][:], in_=x_pairs[1])
        for g in range(G):
            nc.sync.dma_start(out=res[g][:], in_=r[g].rearrange("(p t) n -> p t n", t=HALVES))

        def deal_words(h):
            nc.vector.tensor_copy(
                out=w_dealt[h][:].rearrange("p t (m e) -> p t m e", e=2),
                in_=w_raw[:, h, :].rearrange("p (m t e) -> p t m e", t=HALVES, e=2),
            )

        def deal_scales(h):
            nc.vector.tensor_copy(
                out=s_dealt[h][:],
                in_=s_raw[:, h, :].rearrange("p (m t) -> p t m", t=HALVES),
            )

        def split_bias():
            nc.scalar.copy(out=b_split[:], in_=b_raw[:].rearrange("p (c t) -> p t c", t=HALVES))

        def turn_bias():
            for t in range(HALVES):
                nc.vector.transpose(out=bias[:, t, :], in_=b_split[:, t, :])

        def interleave(h):
            for copy, cols in (
                (nc.vector.tensor_copy, slice(0, VECTOR_COLUMNS[h])),
                (nc.scalar.copy, slice(VECTOR_COLUMNS[h], N)),
            ):
                copy(
                    out=x_bf[h][:, cols, :].rearrange("p (c i) j -> p c j i", i=RUN),
                    in_=x_raw[h][:, :, cols].rearrange("p j (c i) -> p c j i", i=RUN),
                )

        def quantize(h):
            nc.vector.quantize_mx(
                out=x_codes[h][:].bitcast(FP8X4),
                scales=x_scales[h][:],
                in_=x_bf[h][:].rearrange("p n j -> p (n j)"),
            )

        def multiply(h):
            for t in range(HALVES):
                for c in range(SIDE):
                    rows = slice(ROWS * c, ROWS * (c + 1))
                    nc.tensor.matmul_mx(
                        out=acc[SIDE * h + c][t][:],
                        lhsT=w_dealt[h][rows, t, :].bitcast(FP4X4),
                        lhsT_scale=s_dealt[h][rows, t, :],
                        rhs=x_codes[h][rows, :].bitcast(FP8X4),
                        rhs_scale=x_scales[h][rows, :],
                        start=True,
                        stop=True,
                    )

        def finish(g):
            for t in range(HALVES):
                nc.vector.scalar_tensor_tensor(
                    out=y[g][:, t, :],
                    in0=acc[g][t][:],
                    scalar=bias[:, t, B_STEP * g : B_STEP * g + 1],
                    in1=res[g][:, t, :],
                    op0=ADD,
                    op1=ADD,
                )
            nc.sync.dma_start(out=out[g].rearrange("(p t) n -> p t n", t=HALVES), in_=y[g][:])

        interleave(0)
        split_bias()
        deal_words(0)
        deal_scales(0)
        quantize(0)
        multiply(0)
        deal_words(1)
        deal_scales(1)
        interleave(1)
        turn_bias()
        quantize(1)
        multiply(1)
        for g in range(G):
            finish(g)
